import numpy as np, ml_dtypes
CORES = [1,3,5,9,11,13]
N = 6
CB = 128
def setup_inputs(rng):
    return {"x": rng.standard_normal((N, 128, N * CB), dtype=np.float32).astype(ml_dtypes.bfloat16)}
def setup_inputs_big(rng):
    d = setup_inputs(rng)
    for k in ("x",): d[k] = (d[k].astype(np.float32) * 1024.0).astype(d[k].dtype)
    return d
def setup_inputs_small(rng):
    d = setup_inputs(rng)
    for k in ("x",): d[k] = (d[k].astype(np.float32) * (1 / 1024.0)).astype(d[k].dtype)
    return d
def setup_inputs_apart(rng):
    d = setup_inputs(rng)
    f = (10.0 ** rng.permutation(np.linspace(-1.5, 1.5, N))).astype(np.float32).reshape(N, 1, 1)
    for k in ("x",): d[k] = (d[k].astype(np.float32) * f).astype(d[k].dtype)
    return d
def reference(x):
    X = x.astype(np.float64)
    G = sum(X[j].T @ X[j] for j in range(N))
    y = np.full((N, CB, N * CB), np.nan)
    for r in range(N):
        y[r][:, :CB * r] = G[CB * r:CB * r + CB, :CB * r]
    return {"y": y.astype(ml_dtypes.bfloat16 if x.dtype != np.float64 else np.float64)}

@@ -1,0 +1,122 @@
+from concourse.mybir import AluOpType
+
+N = 6
+CB = 128
+SIM_CORES = 16
+BANK = 4
+HELPER_FROM = 5
+
+SCRATCH = {
+    "land": ("sbuf", [128, (N - 1) * CB], "bfloat16"),
+    "yst": ("sbuf", [128, (N - 1) * CB], "bfloat16"),
+}
+for _k in range(3):
+    SCRATCH["xin%d" % _k] = ("sbuf", [128, N * CB], "bfloat16")
+    SCRATCH["out%d" % _k] = ("sbuf", [128, (N - 1) * CB], "bfloat16")
+for _k in range(6):
+    SCRATCH["acc%d" % _k] = ("psum", [128, BANK * CB], "float32")
+
+SEMAPHORES = (["arr%d" % k for k in range(3)] + ["mm%d" % k for k in range(6)] + ["cp%d" % k for k in range(3)]
+              + ["part0", "added", "stored", "sent"])
+
+
+def _bits(mask):
+    return bin(mask).count("1")
+
+
+def _relays(cores, topo):
+    units = []
+    for r in range(N - 1, 0, -1):
+        dst = cores[r]
+        far = [c for c in range(SIM_CORES) if topo.chip(c) != topo.chip(dst)
+               and topo.mates(topo.chip(c), topo.chip(dst)) and topo.may_write(c, dst)]
+        inside = [c for c in far if c in cores]
+        spare = [c for c in far if c not in cores and topo.die(c) == topo.die(dst)]
+        if spare and (r >= HELPER_FROM or not inside):
+            units.append((spare[0], r, 0, r, 0))
+        else:
+            units.append((inside[0], r, 0, r, 0))
+    return units
+
+
+def _jobs(core, cores, units):
+    jobs = [u for u in units if u[0] == core]
+    if core in cores:
+        jobs += [u for u in units if u[1] == cores.index(core)]
+    return jobs
+
+
+def _span(jobs):
+    return min(j[2] for j in jobs), max(j[1] for j in jobs) + 1
+
+
+def rank_program(g, core, T, topo):
+    cores = list(T.cores)
+    units = _relays(cores, topo)
+    mine = _jobs(core, cores, units)
+    rank = T.rank_of(core)
+    if rank is None and not mine:
+        return
+    srcs = [c for c in cores if topo.chip(c) == topo.chip(core)]
+    xin = [T["xin%d" % k] for k in range(len(srcs))]
+    arr = [T.sem["arr%d" % k] for k in range(len(srcs))]
+    sent = 0
+
+    if rank is not None:
+        me = srcs.index(core)
+        g.sync.dma_start(xin[me][:], T.x[:]).then_inc(arr[me], 16)
+        g.wait_ge(arr[me], 16)
+        peers = [d for d in range(SIM_CORES)
+                 if d != core and topo.chip(d) == topo.chip(core) and _jobs(d, cores, units)]
+        relays = [u[0] for u in units]
+        peers.sort(key=lambda d: (d in cores, d not in relays, -_span(_jobs(d, cores, units))[1]))
+        for d in peers:
+            lo, hi = _span(_jobs(d, cores, units))
+            rid, pid, _se = topo.addr(d)
+            m = topo.mask(core, d)
+            g.remote_dma(out_ap=xin[me][:, lo * CB:hi * CB], in_ap=xin[me][:, lo * CB:hi * CB],
+                         remote_sem=arr[me], local_sem=T.sem.sent, pid=pid, routing_id=rid, dma_engine_mask=m)
+            sent += _bits(m)
+
+    banks = []
+    for ji, (_w, r, c0, c1, _p) in enumerate(mine):
+        for b0 in range(c0, c1, BANK):
+            banks.append((ji, r, b0, min(b0 + BANK, c1)))
+
+    order = [k for k in range(len(srcs)) if srcs[k] == core] + [k for k in range(len(srcs)) if srcs[k] != core]
+    if mine:
+        for n, k in enumerate(order):
+            g.tensor.wait_ge(arr[k], 16 if srcs[k] == core else _bits(topo.mask(srcs[k], core)))
+            for b, (_ji, r, b0, b1) in enumerate(banks):
+                g.tensor.matmul(T["acc%d" % b][:, 0:(b1 - b0) * CB], xin[k][:, r * CB:(r + 1) * CB],
+                                xin[k][:, b0 * CB:b1 * CB], n == 0, n == len(order) - 1).then_inc(T.sem["mm%d" % b], 1)
+
+    chunks = [0] * len(mine)
+    for b, (ji, r, b0, b1) in enumerate(banks):
+        w, _r, c0, _c1, p = mine[ji]
+        acc = T["acc%d" % b][:, 0:(b1 - b0) * CB]
+        chunks[ji] += 1
+        g.vector.wait_ge(T.sem["mm%d" % b], len(order))
+        if cores[r] == core:
+            g.vector.wait_ge(T.sem["part%d" % p], _bits(topo.mask(w, core)))
+            g.vector.tensor_tensor(T.yst[:, b0 * CB:b1 * CB], acc, T.land[:, b0 * CB:b1 * CB],
+                                   AluOpType.add).then_inc(T.sem.added, 1)
+        else:
+            g.vector.tensor_copy(T["out%d" % ji][:, (b0 - c0) * CB:(b1 - c0) * CB], acc).then_inc(T.sem["cp%d" % ji], 1)
+
+    for ji, (_w, r, c0, c1, p) in enumerate(mine):
+        if cores[r] == core:
+            continue
+        rid, pid, _se = topo.addr(cores[r])
+        m = topo.mask(core, cores[r])
+        g.wait_ge(T.sem["cp%d" % ji], chunks[ji])
+        g.remote_dma(out_ap=T.land[:, c0 * CB:c1 * CB], in_ap=T["out%d" % ji][:, 0:(c1 - c0) * CB],
+                     remote_sem=T.sem["part%d" % p], local_sem=T.sem.sent, pid=pid, routing_id=rid, dma_engine_mask=m)
+        sent += _bits(m)
+    if sent:
+        g.wait_ge(T.sem.sent, sent)
+
+    if rank:
+        g.sync.wait_ge(T.sem.added, sum(chunks[ji] for ji, j in enumerate(mine) if cores[j[1]] == core))
+        g.sync.dma_start(T.y[:, 0:rank * CB], T.yst[:, 0:rank * CB]).then_inc(T.sem.stored, 16)
+        g.sync.wait_ge(T.sem.stored, 16)

@@ -3,8 +3,8 @@ from concourse.mybir import AluOpType
 N = 6
 CB = 128
 SIM_CORES = 16
-BANK = 4
-HELPER_FROM = 5
+CHUNK = 2
+PIECES = {5: (((0, 1), (1, 3)), ((3, 4), (4, 5)))}
 
 SCRATCH = {
     "land": ("sbuf", [128, (N - 1) * CB], "bfloat16"),
@@ -13,11 +13,11 @@ SCRATCH = {
 for _k in range(3):
     SCRATCH["xin%d" % _k] = ("sbuf", [128, N * CB], "bfloat16")
     SCRATCH["out%d" % _k] = ("sbuf", [128, (N - 1) * CB], "bfloat16")
-for _k in range(6):
-    SCRATCH["acc%d" % _k] = ("psum", [128, BANK * CB], "float32")
+for _k in range(8):
+    SCRATCH["acc%d" % _k] = ("psum", [128, 512], "float32")
 
-SEMAPHORES = (["arr%d" % k for k in range(3)] + ["mm%d" % k for k in range(6)] + ["cp%d" % k for k in range(3)]
-              + ["part0", "added", "stored", "sent"])
+SEMAPHORES = (["arr%d" % k for k in range(3)] + ["mm%d" % k for k in range(8)] + ["cp%d" % k for k in range(3)]
+              + ["part%d" % k for k in range(4)] + ["added0", "added1", "stored0", "stored1", "sent"])
 
 
 def _bits(mask):
@@ -25,98 +25,126 @@ def _bits(mask):
 
 
 def _relays(cores, topo):
-    units = []
+    units, taken = [], []
     for r in range(N - 1, 0, -1):
         dst = cores[r]
-        far = [c for c in range(SIM_CORES) if topo.chip(c) != topo.chip(dst)
-               and topo.mates(topo.chip(c), topo.chip(dst)) and topo.may_write(c, dst)]
+        far = [c for c in range(SIM_CORES) if topo.mates(topo.chip(c), topo.chip(dst)) and topo.may_write(c, dst)]
         inside = [c for c in far if c in cores]
-        spare = [c for c in far if c not in cores and topo.die(c) == topo.die(dst)]
-        if spare and (r >= HELPER_FROM or not inside):
-            units.append((spare[0], r, 0, r, 0))
+        spare = [c for c in far if c not in cores and c not in taken and topo.die(c) == topo.die(dst)]
+        if r in PIECES and len(spare) >= len(PIECES[r]):
+            p = 0
+            for s, pieces in enumerate(PIECES[r]):
+                taken.append(spare[s])
+                for t, (c0, c1) in enumerate(pieces):
+                    units.append((spare[s], r, c0, c1, p, s, t))
+                    p += 1
         else:
-            units.append((inside[0], r, 0, r, 0))
+            units.append(((inside + spare)[0], r, 0, r, 0, 0, 0))
     return units
 
 
 def _jobs(core, cores, units):
-    jobs = [u for u in units if u[0] == core]
-    if core in cores:
-        jobs += [u for u in units if u[1] == cores.index(core)]
-    return jobs
+    return ([("sum", u) for u in units if u[0] == core]
+            + [("own", u) for u in sorted([u for u in units if cores[u[1]] == core], key=lambda u: (u[6], u[5]))])
 
 
 def _span(jobs):
-    return min(j[2] for j in jobs), max(j[1] for j in jobs) + 1
+    return min(u[2] for kind, u in jobs), max(u[1] for kind, u in jobs) + 1
+
+
+def _peers(sender, cores, units, topo):
+    relays = [u[0] for u in units]
+    peers = [d for d in range(SIM_CORES)
+             if d != sender and topo.chip(d) == topo.chip(sender) and _jobs(d, cores, units)]
+    peers.sort(key=lambda d: (d not in relays, d not in cores, relays.index(d) if d in relays else -cores.index(d)))
+    return [(d,) + _span(_jobs(d, cores, units)) for d in peers]
+
+
+def _ahead(sender, dst, cores, units, topo):
+    n = 0
+    for d, lo, hi in _peers(sender, cores, units, topo):
+        if d == dst:
+            break
+        n += hi - lo
+    return n
 
 
 def rank_program(g, core, T, topo):
     cores = list(T.cores)
     units = _relays(cores, topo)
-    mine = _jobs(core, cores, units)
     rank = T.rank_of(core)
+    mine = _jobs(core, cores, units)
     if rank is None and not mine:
         return
     srcs = [c for c in cores if topo.chip(c) == topo.chip(core)]
     xin = [T["xin%d" % k] for k in range(len(srcs))]
     arr = [T.sem["arr%d" % k] for k in range(len(srcs))]
-    sent = 0
+    sent = [0]
+
+    def write(dst, out_ap, in_ap, sem):
+        rid, pid, _se = topo.addr(dst)
+        m = topo.mask(core, dst)
+        g.remote_dma(out_ap=out_ap, in_ap=in_ap, remote_sem=sem, local_sem=T.sem.sent, pid=pid, routing_id=rid,
+                     dma_engine_mask=m)
+        sent[0] += _bits(m)
 
     if rank is not None:
         me = srcs.index(core)
         g.sync.dma_start(xin[me][:], T.x[:]).then_inc(arr[me], 16)
         g.wait_ge(arr[me], 16)
-        peers = [d for d in range(SIM_CORES)
-                 if d != core and topo.chip(d) == topo.chip(core) and _jobs(d, cores, units)]
-        relays = [u[0] for u in units]
-        peers.sort(key=lambda d: (d in cores, d not in relays, -_span(_jobs(d, cores, units))[1]))
-        for d in peers:
-            lo, hi = _span(_jobs(d, cores, units))
-            rid, pid, _se = topo.addr(d)
-            m = topo.mask(core, d)
-            g.remote_dma(out_ap=xin[me][:, lo * CB:hi * CB], in_ap=xin[me][:, lo * CB:hi * CB],
-                         remote_sem=arr[me], local_sem=T.sem.sent, pid=pid, routing_id=rid, dma_engine_mask=m)
-            sent += _bits(m)
+        for d, lo, hi in _peers(core, cores, units, topo):
+            write(d, xin[me][:, lo * CB:hi * CB], xin[me][:, lo * CB:hi * CB], arr[me])
 
     banks = []
-    for ji, (_w, r, c0, c1, _p) in enumerate(mine):
-        for b0 in range(c0, c1, BANK):
-            banks.append((ji, r, b0, min(b0 + BANK, c1)))
+    for ji, (_kind, u) in enumerate(mine):
+        for b0 in range(u[2], u[3], CHUNK):
+            banks.append((ji, u[1], b0, min(b0 + CHUNK, u[3])))
 
-    order = [k for k in range(len(srcs)) if srcs[k] == core] + [k for k in range(len(srcs)) if srcs[k] != core]
-    if mine:
-        for n, k in enumerate(order):
+    wait = [-1 if s == core else _ahead(s, core, cores, units, topo) for s in srcs]
+    order = sorted(range(len(srcs)), key=lambda k: (wait[k], k))
+    head = order[:1] if wait[order[0]] < wait[order[1]] else []
+    seen = []
+
+    def mm(b, k):
+        if k not in seen:
+            seen.append(k)
             g.tensor.wait_ge(arr[k], 16 if srcs[k] == core else _bits(topo.mask(srcs[k], core)))
-            for b, (_ji, r, b0, b1) in enumerate(banks):
-                g.tensor.matmul(T["acc%d" % b][:, 0:(b1 - b0) * CB], xin[k][:, r * CB:(r + 1) * CB],
-                                xin[k][:, b0 * CB:b1 * CB], n == 0, n == len(order) - 1).then_inc(T.sem["mm%d" % b], 1)
+        _ji, r, b0, b1 = banks[b]
+        g.tensor.matmul(T["acc%d" % b][:, 0:(b1 - b0) * CB], xin[k][:, r * CB:(r + 1) * CB],
+                        xin[k][:, b0 * CB:b1 * CB], k == order[0], k == order[-1]).then_inc(T.sem["mm%d" % b], 1)
+
+    for k in head:
+        for b in range(len(banks)):
+            mm(b, k)
+    for b in range(len(banks)):
+        for k in order:
+            if k not in head:
+                mm(b, k)
 
     chunks = [0] * len(mine)
     for b, (ji, r, b0, b1) in enumerate(banks):
-        w, _r, c0, _c1, p = mine[ji]
+        kind, (w, _r, c0, _c1, p, s, _t) = mine[ji]
         acc = T["acc%d" % b][:, 0:(b1 - b0) * CB]
         chunks[ji] += 1
-        g.vector.wait_ge(T.sem["mm%d" % b], len(order))
-        if cores[r] == core:
+        g.vector.wait_ge(T.sem["mm%d" % b], len(srcs))
+        if kind == "own":
             g.vector.wait_ge(T.sem["part%d" % p], _bits(topo.mask(w, core)))
             g.vector.tensor_tensor(T.yst[:, b0 * CB:b1 * CB], acc, T.land[:, b0 * CB:b1 * CB],
-                                   AluOpType.add).then_inc(T.sem.added, 1)
+                                   AluOpType.add).then_inc(T.sem["added%d" % s], 1)
         else:
             g.vector.tensor_copy(T["out%d" % ji][:, (b0 - c0) * CB:(b1 - c0) * CB], acc).then_inc(T.sem["cp%d" % ji], 1)
 
-    for ji, (_w, r, c0, c1, p) in enumerate(mine):
-        if cores[r] == core:
-            continue
-        rid, pid, _se = topo.addr(cores[r])
-        m = topo.mask(core, cores[r])
-        g.wait_ge(T.sem["cp%d" % ji], chunks[ji])
-        g.remote_dma(out_ap=T.land[:, c0 * CB:c1 * CB], in_ap=T["out%d" % ji][:, 0:(c1 - c0) * CB],
-                     remote_sem=T.sem["part%d" % p], local_sem=T.sem.sent, pid=pid, routing_id=rid, dma_engine_mask=m)
-        sent += _bits(m)
-    if sent:
-        g.wait_ge(T.sem.sent, sent)
+    for ji, (kind, (w, r, c0, c1, p, _s, _t)) in enumerate(mine):
+        if kind == "sum":
+            g.wait_ge(T.sem["cp%d" % ji], chunks[ji])
+            write(cores[r], T.land[:, c0 * CB:c1 * CB], T["out%d" % ji][:, 0:(c1 - c0) * CB], T.sem["part%d" % p])
+    if sent[0]:
+        g.wait_ge(T.sem.sent, sent[0])
 
-    if rank:
-        g.sync.wait_ge(T.sem.added, sum(chunks[ji] for ji, j in enumerate(mine) if cores[j[1]] == core))
-        g.sync.dma_start(T.y[:, 0:rank * CB], T.yst[:, 0:rank * CB]).then_inc(T.sem.stored, 16)
-        g.sync.wait_ge(T.sem.stored, 16)
+    own = [(ji, u) for ji, (kind, u) in enumerate(mine) if kind == "own"]
+    for s in sorted({u[5] for ji, u in own}):
+        q = (g.sync, g.scalar)[s]
+        lo, hi = min(u[2] for ji, u in own if u[5] == s), max(u[3] for ji, u in own if u[5] == s)
+        q.wait_ge(T.sem["added%d" % s], sum(chunks[ji] for ji, u in own if u[5] == s))
+        q.dma_start(T.y[:, lo * CB:hi * CB], T.yst[:, lo * CB:hi * CB]).then_inc(T.sem["stored%d" % s], 16)
+        q.wait_ge(T.sem["stored%d" % s], 16)

@@ -4,81 +4,130 @@ N = 6
 CB = 128
 SIM_CORES = 16
 CHUNK = 2
-PIECES = {5: (((0, 1), (1, 3)), ((3, 4), (4, 5)))}
+UNITS = ((1, 5, 0, 1), (1, 5, 1, 3), (2, 4, 3, 4), (2, 5, 3, 5), (0, 4, 0, 3), (0, 3, 0, 3), (0, 2, 0, 2), (0, 1, 0, 1))
 
 SCRATCH = {
     "land": ("sbuf", [128, (N - 1) * CB], "bfloat16"),
     "yst": ("sbuf", [128, (N - 1) * CB], "bfloat16"),
 }
 for _k in range(3):
-    SCRATCH["xin%d" % _k] = ("sbuf", [128, N * CB], "bfloat16")
+    SCRATCH["xin%d" % _k] = ("sbuf", [128, (N + 1) * CB], "bfloat16")
     SCRATCH["out%d" % _k] = ("sbuf", [128, (N - 1) * CB], "bfloat16")
 for _k in range(8):
     SCRATCH["acc%d" % _k] = ("psum", [128, 512], "float32")
 
-SEMAPHORES = (["arr%d" % k for k in range(3)] + ["mm%d" % k for k in range(8)] + ["cp%d" % k for k in range(3)]
-              + ["part%d" % k for k in range(4)] + ["added0", "added1", "stored0", "stored1", "sent"])
+SEMAPHORES = (["ld%d" % k for k in range(4)] + ["a%d%d" % (k, s) for k in range(3) for s in range(2)]
+              + ["mm%d" % k for k in range(8)] + ["cp%d" % k for k in range(3)] + ["part%d" % k for k in range(3)]
+              + ["added0", "added1", "stored0", "stored1", "sent"])
 
 
 def _bits(mask):
     return bin(mask).count("1")
 
 
-def _relays(cores, topo):
-    units, taken = [], []
-    for r in range(N - 1, 0, -1):
+def _units(cores, topo):
+    raw = []
+    for role, r, c0, c1 in UNITS:
         dst = cores[r]
         far = [c for c in range(SIM_CORES) if topo.mates(topo.chip(c), topo.chip(dst)) and topo.may_write(c, dst)]
         inside = [c for c in far if c in cores]
-        spare = [c for c in far if c not in cores and c not in taken and topo.die(c) == topo.die(dst)]
-        if r in PIECES and len(spare) >= len(PIECES[r]):
-            p = 0
-            for s, pieces in enumerate(PIECES[r]):
-                taken.append(spare[s])
-                for t, (c0, c1) in enumerate(pieces):
-                    units.append((spare[s], r, c0, c1, p, s, t))
-                    p += 1
-        else:
-            units.append(((inside + spare)[0], r, 0, r, 0, 0, 0))
+        spare = sorted([c for c in far if c not in cores], key=lambda c: (topo.die(c) != topo.die(cores[N - 1]), c))
+        raw.append(((inside + spare)[0] if role == 0 else spare[role - 1], r, c0, c1))
+    units = []
+    for u in raw:
+        row = sorted([v for v in raw if v[1] == u[1]], key=lambda v: v[2])
+        ws = []
+        for v in row:
+            if v[0] not in ws:
+                ws.append(v[0])
+        units.append(u + (row.index(u), ws.index(u[0])))
     return units
 
 
 def _jobs(core, cores, units):
     return ([("sum", u) for u in units if u[0] == core]
-            + [("own", u) for u in sorted([u for u in units if cores[u[1]] == core], key=lambda u: (u[6], u[5]))])
+            + [("own", u) for u in sorted([u for u in units if cores[u[1]] == core], key=lambda u: u[2])])
 
 
-def _span(jobs):
-    return min(u[2] for kind, u in jobs), max(u[1] for kind, u in jobs) + 1
+def _slot(dup, r):
+    return 0 if dup and r == N - 1 else r + 1
 
 
-def _peers(sender, cores, units, topo):
+def _hull(jobs, dup):
+    s = []
+    for _kind, u in jobs:
+        s += [_slot(dup, u[1]), u[2] + 1, u[3]]
+    return min(s), max(s) + 1
+
+
+def _stages(jobs):
+    nat, alt = _hull(jobs, False), _hull(jobs, True)
+    dup = alt[1] - alt[0] < nat[1] - nat[0]
+    lo, hi = _hull(jobs, dup)
+    l1, h1 = _hull(jobs[:1], dup)
+    if l1 == lo and hi - h1 >= 2:
+        return dup, [(lo, h1), (h1, hi)]
+    return dup, [(lo, hi)]
+
+
+def _stage_of(stages, dup, r, b0, b1):
+    need = [_slot(dup, r)] + list(range(b0 + 1, b1 + 1))
+    return max(s for s, (lo, hi) in enumerate(stages) if any(lo <= i < hi for i in need))
+
+
+def _deliv(sender, cores, units, topo):
     relays = [u[0] for u in units]
-    peers = [d for d in range(SIM_CORES)
-             if d != sender and topo.chip(d) == topo.chip(sender) and _jobs(d, cores, units)]
-    peers.sort(key=lambda d: (d not in relays, d not in cores, relays.index(d) if d in relays else -cores.index(d)))
-    return [(d,) + _span(_jobs(d, cores, units)) for d in peers]
+    out = []
+    for d in range(SIM_CORES):
+        jobs = _jobs(d, cores, units)
+        if d == sender or topo.chip(d) != topo.chip(sender) or not jobs:
+            continue
+        dup, stages = _stages(jobs)
+        for s, (lo, hi) in enumerate(stages):
+            forsum = any(kind == "sum" and _stage_of(stages, dup, u[1], u[2], u[3]) == s for kind, u in jobs)
+            key = (0, s, d in cores, relays.index(d)) if forsum else (1, -cores.index(d), s, 0)
+            out.append((key, d, s, lo, hi))
+    out.sort()
+    return [t[1:] for t in out]
 
 
-def _ahead(sender, dst, cores, units, topo):
+def _ahead(sender, dst, stage, cores, units, topo):
     n = 0
-    for d, lo, hi in _peers(sender, cores, units, topo):
-        if d == dst:
-            break
+    for d, s, lo, hi in _deliv(sender, cores, units, topo):
         n += hi - lo
+        if d == dst and s == stage:
+            break
     return n
+
+
+def _loads(core, cores, units, topo):
+    jobs = _jobs(core, cores, units)
+    spans = [(lo, hi) for _d, _s, lo, hi in _deliv(core, cores, units, topo)] + (_stages(jobs)[1] if jobs else [])
+    have, pieces = [], []
+    for lo, hi in spans:
+        run = []
+        for i in range(lo, hi):
+            if i in have:
+                continue
+            have.append(i)
+            if run and (i != run[-1] + 1 or run[-1] == 0):
+                pieces.append((run[0], run[-1] + 1))
+                run = []
+            run.append(i)
+        if run:
+            pieces.append((run[0], run[-1] + 1))
+    return pieces
 
 
 def rank_program(g, core, T, topo):
     cores = list(T.cores)
-    units = _relays(cores, topo)
+    units = _units(cores, topo)
     rank = T.rank_of(core)
     mine = _jobs(core, cores, units)
     if rank is None and not mine:
         return
     srcs = [c for c in cores if topo.chip(c) == topo.chip(core)]
     xin = [T["xin%d" % k] for k in range(len(srcs))]
-    arr = [T.sem["arr%d" % k] for k in range(len(srcs))]
     sent = [0]
 
     def write(dst, out_ap, in_ap, sem):
@@ -88,56 +137,74 @@ def rank_program(g, core, T, topo):
                      dma_engine_mask=m)
         sent[0] += _bits(m)
 
+    pieces = []
     if rank is not None:
         me = srcs.index(core)
-        g.sync.dma_start(xin[me][:], T.x[:]).then_inc(arr[me], 16)
-        g.wait_ge(arr[me], 16)
-        for d, lo, hi in _peers(core, cores, units, topo):
-            write(d, xin[me][:, lo * CB:hi * CB], xin[me][:, lo * CB:hi * CB], arr[me])
+        pieces = _loads(core, cores, units, topo)
+        for i, (lo, hi) in enumerate(pieces):
+            c0 = N - 1 if lo == 0 else lo - 1
+            (g.sync, g.scalar)[i % 2].dma_start(xin[me][:, lo * CB:hi * CB],
+                                                T.x[:, c0 * CB:(c0 + hi - lo) * CB]).then_inc(T.sem["ld%d" % i], 16)
+        got = []
+        for d, s, lo, hi in _deliv(core, cores, units, topo):
+            for i, (p0, p1) in enumerate(pieces):
+                if p0 < hi and lo < p1 and i not in got:
+                    got.append(i)
+                    g.wait_ge(T.sem["ld%d" % i], 16)
+            write(d, xin[me][:, lo * CB:hi * CB], xin[me][:, lo * CB:hi * CB], T.sem["a%d%d" % (me, s)])
 
-    banks = []
-    for ji, (_kind, u) in enumerate(mine):
-        for b0 in range(u[2], u[3], CHUNK):
-            banks.append((ji, u[1], b0, min(b0 + CHUNK, u[3])))
+    if mine:
+        dup, stages = _stages(mine)
 
-    wait = [-1 if s == core else _ahead(s, core, cores, units, topo) for s in srcs]
-    order = sorted(range(len(srcs)), key=lambda k: (wait[k], k))
-    head = order[:1] if wait[order[0]] < wait[order[1]] else []
-    seen = []
+        banks = []
+        for ji, (_kind, u) in enumerate(mine):
+            for b0 in range(u[2], u[3], CHUNK):
+                b1 = min(b0 + CHUNK, u[3])
+                banks.append((ji, u[1], b0, b1, _stage_of(stages, dup, u[1], b0, b1)))
 
-    def mm(b, k):
-        if k not in seen:
-            seen.append(k)
-            g.tensor.wait_ge(arr[k], 16 if srcs[k] == core else _bits(topo.mask(srcs[k], core)))
-        _ji, r, b0, b1 = banks[b]
-        g.tensor.matmul(T["acc%d" % b][:, 0:(b1 - b0) * CB], xin[k][:, r * CB:(r + 1) * CB],
-                        xin[k][:, b0 * CB:b1 * CB], k == order[0], k == order[-1]).then_inc(T.sem["mm%d" % b], 1)
+        tasks = []
+        for b, (_ji, _r, _b0, _b1, st) in enumerate(banks):
+            for k, s in enumerate(srcs):
+                tasks.append((-1 if s == core else _ahead(s, core, st, cores, units, topo), b, k))
+        tasks.sort()
+        seen, done = [], [0] * len(banks)
+        for _av, b, k in tasks:
+            _ji, r, b0, b1, st = banks[b]
+            if srcs[k] == core:
+                if "own" not in seen:
+                    seen.append("own")
+                    for i in range(len(pieces)):
+                        g.tensor.wait_ge(T.sem["ld%d" % i], 16)
+            else:
+                for s in range(st + 1):
+                    if (k, s) not in seen:
+                        seen.append((k, s))
+                        g.tensor.wait_ge(T.sem["a%d%d" % (k, s)], _bits(topo.mask(srcs[k], core)))
+            done[b] += 1
+            li = _slot(dup, r)
+            g.tensor.matmul(T["acc%d" % b][:, 0:(b1 - b0) * CB], xin[k][:, li * CB:(li + 1) * CB],
+                            xin[k][:, (b0 + 1) * CB:(b1 + 1) * CB], done[b] == 1,
+                            done[b] == len(srcs)).then_inc(T.sem["mm%d" % b], 1)
 
-    for k in head:
-        for b in range(len(banks)):
-            mm(b, k)
-    for b in range(len(banks)):
-        for k in order:
-            if k not in head:
-                mm(b, k)
+        chunks = [0] * len(mine)
+        for b, (ji, r, b0, b1, _st) in enumerate(banks):
+            kind, (w, _r, c0, _c1, p, s) = mine[ji]
+            acc = T["acc%d" % b][:, 0:(b1 - b0) * CB]
+            chunks[ji] += 1
+            g.vector.wait_ge(T.sem["mm%d" % b], len(srcs))
+            if kind == "own":
+                g.vector.wait_ge(T.sem["part%d" % p], _bits(topo.mask(w, core)))
+                g.vector.tensor_tensor(T.yst[:, b0 * CB:b1 * CB], acc, T.land[:, b0 * CB:b1 * CB],
+                                       AluOpType.add).then_inc(T.sem["added%d" % s], 1)
+            else:
+                g.vector.tensor_copy(T["out%d" % ji][:, (b0 - c0) * CB:(b1 - c0) * CB],
+                                     acc).then_inc(T.sem["cp%d" % ji], 1)
 
-    chunks = [0] * len(mine)
-    for b, (ji, r, b0, b1) in enumerate(banks):
-        kind, (w, _r, c0, _c1, p, s, _t) = mine[ji]
-        acc = T["acc%d" % b][:, 0:(b1 - b0) * CB]
-        chunks[ji] += 1
-        g.vector.wait_ge(T.sem["mm%d" % b], len(srcs))
-        if kind == "own":
-            g.vector.wait_ge(T.sem["part%d" % p], _bits(topo.mask(w, core)))
-            g.vector.tensor_tensor(T.yst[:, b0 * CB:b1 * CB], acc, T.land[:, b0 * CB:b1 * CB],
-                                   AluOpType.add).then_inc(T.sem["added%d" % s], 1)
-        else:
-            g.vector.tensor_copy(T["out%d" % ji][:, (b0 - c0) * CB:(b1 - c0) * CB], acc).then_inc(T.sem["cp%d" % ji], 1)
+        for ji, (kind, (w, r, c0, c1, p, _s)) in enumerate(mine):
+            if kind == "sum":
+                g.wait_ge(T.sem["cp%d" % ji], chunks[ji])
+                write(cores[r], T.land[:, c0 * CB:c1 * CB], T["out%d" % ji][:, 0:(c1 - c0) * CB], T.sem["part%d" % p])
 
-    for ji, (kind, (w, r, c0, c1, p, _s, _t)) in enumerate(mine):
-        if kind == "sum":
-            g.wait_ge(T.sem["cp%d" % ji], chunks[ji])
-            write(cores[r], T.land[:, c0 * CB:c1 * CB], T["out%d" % ji][:, 0:(c1 - c0) * CB], T.sem["part%d" % p])
     if sent[0]:
         g.wait_ge(T.sem.sent, sent[0])
 

from concourse.mybir import AluOpType

N = 6
CB = 128
SIM_CORES = 16
CHUNK = 2
UNITS = ((1, 5, 0, 1), (1, 5, 1, 3), (2, 4, 3, 4), (2, 5, 3, 5), (0, 4, 0, 3), (0, 3, 0, 3), (0, 2, 0, 2), (0, 1, 0, 1))

SCRATCH = {
    "land": ("sbuf", [128, (N - 1) * CB], "bfloat16"),
    "yst": ("sbuf", [128, (N - 1) * CB], "bfloat16"),
}
for _k in range(3):
    SCRATCH["xin%d" % _k] = ("sbuf", [128, (N + 1) * CB], "bfloat16")
    SCRATCH["out%d" % _k] = ("sbuf", [128, (N - 1) * CB], "bfloat16")
for _k in range(8):
    SCRATCH["acc%d" % _k] = ("psum", [128, 512], "float32")

SEMAPHORES = (["ld%d" % k for k in range(4)] + ["a%d%d" % (k, s) for k in range(3) for s in range(2)]
              + ["mm%d" % k for k in range(8)] + ["cp%d" % k for k in range(3)] + ["part%d" % k for k in range(3)]
              + ["added0", "added1", "stored0", "stored1", "sent"])


def _bits(mask):
    return bin(mask).count("1")


def _units(cores, topo):
    raw = []
    for role, r, c0, c1 in UNITS:
        dst = cores[r]
        far = [c for c in range(SIM_CORES) if topo.mates(topo.chip(c), topo.chip(dst)) and topo.may_write(c, dst)]
        inside = [c for c in far if c in cores]
        spare = sorted([c for c in far if c not in cores], key=lambda c: (topo.die(c) != topo.die(cores[N - 1]), c))
        raw.append(((inside + spare)[0] if role == 0 else spare[role - 1], r, c0, c1))
    units = []
    for u in raw:
        row = sorted([v for v in raw if v[1] == u[1]], key=lambda v: v[2])
        ws = []
        for v in row:
            if v[0] not in ws:
                ws.append(v[0])
        units.append(u + (row.index(u), ws.index(u[0])))
    return units


def _jobs(core, cores, units):
    return ([("sum", u) for u in units if u[0] == core]
            + [("own", u) for u in sorted([u for u in units if cores[u[1]] == core], key=lambda u: u[2])])


def _slot(dup, r):
    return 0 if dup and r == N - 1 else r + 1


def _hull(jobs, dup):
    s = []
    for _kind, u in jobs:
        s += [_slot(dup, u[1]), u[2] + 1, u[3]]
    return min(s), max(s) + 1


def _stages(jobs):
    nat, alt = _hull(jobs, False), _hull(jobs, True)
    dup = alt[1] - alt[0] < nat[1] - nat[0]
    lo, hi = _hull(jobs, dup)
    l1, h1 = _hull(jobs[:1], dup)
    if l1 == lo and hi - h1 >= 2:
        return dup, [(lo, h1), (h1, hi)]
    return dup, [(lo, hi)]


def _stage_of(stages, dup, r, b0, b1):
    need = [_slot(dup, r)] + list(range(b0 + 1, b1 + 1))
    return max(s for s, (lo, hi) in enumerate(stages) if any(lo <= i < hi for i in need))


def _deliv(sender, cores, units, topo):
    relays = [u[0] for u in units]
    out = []
    for d in range(SIM_CORES):
        jobs = _jobs(d, cores, units)
        if d == sender or topo.chip(d) != topo.chip(sender) or not jobs:
            continue
        dup, stages = _stages(jobs)
        for s, (lo, hi) in enumerate(stages):
            forsum = any(kind == "sum" and _stage_of(stages, dup, u[1], u[2], u[3]) == s for kind, u in jobs)
            key = (0, s, d in cores, relays.index(d)) if forsum else (1, -cores.index(d), s, 0)
            out.append((key, d, s, lo, hi))
    out.sort()
    return [t[1:] for t in out]


def _ahead(sender, dst, stage, cores, units, topo):
    n = 0
    for d, s, lo, hi in _deliv(sender, cores, units, topo):
        n += hi - lo
        if d == dst and s == stage:
            break
    return n


def _loads(core, cores, units, topo):
    jobs = _jobs(core, cores, units)
    spans = [(lo, hi) for _d, _s, lo, hi in _deliv(core, cores, units, topo)] + (_stages(jobs)[1] if jobs else [])
    have, pieces = [], []
    for lo, hi in spans:
        run = []
        for i in range(lo, hi):
            if i in have:
                continue
            have.append(i)
            if run and (i != run[-1] + 1 or run[-1] == 0):
                pieces.append((run[0], run[-1] + 1))
                run = []
            run.append(i)
        if run:
            pieces.append((run[0], run[-1] + 1))
    return pieces


def rank_program(g, core, T, topo):
    cores = list(T.cores)
    units = _units(cores, topo)
    rank = T.rank_of(core)
    mine = _jobs(core, cores, units)
    if rank is None and not mine:
        return
    srcs = [c for c in cores if topo.chip(c) == topo.chip(core)]
    xin = [T["xin%d" % k] for k in range(len(srcs))]
    sent = [0]

    def write(dst, out_ap, in_ap, sem):
        rid, pid, _se = topo.addr(dst)
        m = topo.mask(core, dst)
        g.remote_dma(out_ap=out_ap, in_ap=in_ap, remote_sem=sem, local_sem=T.sem.sent, pid=pid, routing_id=rid,
                     dma_engine_mask=m)
        sent[0] += _bits(m)

    pieces = []
    if rank is not None:
        me = srcs.index(core)
        pieces = _loads(core, cores, units, topo)
        for i, (lo, hi) in enumerate(pieces):
            c0 = N - 1 if lo == 0 else lo - 1
            (g.sync, g.scalar)[i % 2].dma_start(xin[me][:, lo * CB:hi * CB],
                                                T.x[:, c0 * CB:(c0 + hi - lo) * CB]).then_inc(T.sem["ld%d" % i], 16)
        got = []
        for d, s, lo, hi in _deliv(core, cores, units, topo):
            for i, (p0, p1) in enumerate(pieces):
                if p0 < hi and lo < p1 and i not in got:
                    got.append(i)
                    g.wait_ge(T.sem["ld%d" % i], 16)
            write(d, xin[me][:, lo * CB:hi * CB], xin[me][:, lo * CB:hi * CB], T.sem["a%d%d" % (me, s)])

    if mine:
        dup, stages = _stages(mine)

        banks = []
        for ji, (_kind, u) in enumerate(mine):
            for b0 in range(u[2], u[3], CHUNK):
                b1 = min(b0 + CHUNK, u[3])
                banks.append((ji, u[1], b0, b1, _stage_of(stages, dup, u[1], b0, b1)))

        tasks = []
        for b, (_ji, _r, _b0, _b1, st) in enumerate(banks):
            for k, s in enumerate(srcs):
                tasks.append((-1 if s == core else _ahead(s, core, st, cores, units, topo), b, k))
        tasks.sort()
        seen, done = [], [0] * len(banks)
        for _av, b, k in tasks:
            _ji, r, b0, b1, st = banks[b]
            if srcs[k] == core:
                if "own" not in seen:
                    seen.append("own")
                    for i in range(len(pieces)):
                        g.tensor.wait_ge(T.sem["ld%d" % i], 16)
            else:
                for s in range(st + 1):
                    if (k, s) not in seen:
                        seen.append((k, s))
                        g.tensor.wait_ge(T.sem["a%d%d" % (k, s)], _bits(topo.mask(srcs[k], core)))
            done[b] += 1
            li = _slot(dup, r)
            g.tensor.matmul(T["acc%d" % b][:, 0:(b1 - b0) * CB], xin[k][:, li * CB:(li + 1) * CB],
                            xin[k][:, (b0 + 1) * CB:(b1 + 1) * CB], done[b] == 1,
                            done[b] == len(srcs)).then_inc(T.sem["mm%d" % b], 1)

        chunks = [0] * len(mine)
        for b, (ji, r, b0, b1, _st) in enumerate(banks):
            kind, (w, _r, c0, _c1, p, s) = mine[ji]
            acc = T["acc%d" % b][:, 0:(b1 - b0) * CB]
            chunks[ji] += 1
            g.vector.wait_ge(T.sem["mm%d" % b], len(srcs))
            if kind == "own":
                g.vector.wait_ge(T.sem["part%d" % p], _bits(topo.mask(w, core)))
                g.vector.tensor_tensor(T.yst[:, b0 * CB:b1 * CB], acc, T.land[:, b0 * CB:b1 * CB],
                                       AluOpType.add).then_inc(T.sem["added%d" % s], 1)
            else:
                g.vector.tensor_copy(T["out%d" % ji][:, (b0 - c0) * CB:(b1 - c0) * CB],
                                     acc).then_inc(T.sem["cp%d" % ji], 1)

        for ji, (kind, (w, r, c0, c1, p, _s)) in enumerate(mine):
            if kind == "sum":
                g.wait_ge(T.sem["cp%d" % ji], chunks[ji])
                write(cores[r], T.land[:, c0 * CB:c1 * CB], T["out%d" % ji][:, 0:(c1 - c0) * CB], T.sem["part%d" % p])

    if sent[0]:
        g.wait_ge(T.sem.sent, sent[0])

    own = [(ji, u) for ji, (kind, u) in enumerate(mine) if kind == "own"]
    for s in sorted({u[5] for ji, u in own}):
        q = (g.sync, g.scalar)[s]
        lo, hi = min(u[2] for ji, u in own if u[5] == s), max(u[3] for ji, u in own if u[5] == s)
        q.wait_ge(T.sem["added%d" % s], sum(chunks[ji] for ji, u in own if u[5] == s))
        q.dma_start(T.y[:, lo * CB:hi * CB], T.yst[:, lo * CB:hi * CB]).then_inc(T.sem["stored%d" % s], 16)
        q.wait_ge(T.sem["stored%d" % s], 16)
